import numpy as np
import ml_dtypes


def mxq(x, axis, fmt="e4m3"):
    dtype, down = {"e4m3": (ml_dtypes.float8_e4m3fn, 7), "e5m2": (ml_dtypes.float8_e5m2, 14)}[fmt]
    v = np.moveaxis(np.asarray(x, np.float32).astype(ml_dtypes.bfloat16).astype(np.float64), axis, -1)
    blocks = v.reshape(v.shape[:-1] + (-1, 32))
    amax = np.abs(blocks).max(-1, keepdims=True)
    byte = np.maximum(np.where(amax > 0, np.frexp(amax)[1] - 1 + 127, 0) - down, 1)
    scale = np.exp2(byte - 127.0)
    codes = (blocks / scale).astype(np.float32).astype(dtype).astype(np.float64)
    return np.moveaxis((codes * scale).reshape(v.shape), -1, axis)


WIDE = False


def mx_kscale(k):
    if not WIDE:
        return np.ones(k)
    levels = np.array([10, -10, 5, -5, 0])
    if k % 512:
        return np.exp2(np.random.permutation(np.resize(levels, k // 32))).repeat(32)
    a = np.empty((k // 512, 16))
    for p in range(k // 512):
        a[p, :8] = np.random.permutation(np.resize(levels, 8))
        for g in range(8):
            far = levels[np.abs(levels - a[p, g]) >= 10]
            a[p, g + 8] = far[np.random.randint(len(far))]
    return np.exp2(a.ravel()).repeat(32)


def f64(x):
    return np.asarray(x).astype(np.float64)


def striped(idx):
    return np.tile(idx.reshape(-1, 16).T, (8, 1)).astype(np.uint16)


def unstriped(offs):
    return offs[:16].T.reshape(-1).astype(np.int64)


E2M1 = np.array([0.0, 0.5, 1.0, 1.5, 2.0, 3.0, 4.0, 6.0, -0.0, -0.5, -1.0, -1.5, -2.0, -3.0, -4.0, -6.0])


def pack_weight(w, fmt):
    k, n = w.shape
    w = f64(np.asarray(w, np.float32).astype(ml_dtypes.bfloat16)).reshape(k // 32, 32, n)
    amax = np.abs(w).max(1)
    if fmt == "e4m3":
        byte = np.frexp(amax)[1] - 1 + 127 - 7
    else:
        mant, ex = np.frexp(amax / 6.0)
        byte = np.where(mant > 0.5, ex, ex - 1) + 127
    byte = np.clip(np.where(amax > 0, byte, 1), 1, 254)
    scaled = (w * np.exp2(127.0 - byte)[:, None, :]).reshape(k, n).astype(np.float32)
    by_word = np.ascontiguousarray(scaled.reshape(k // 512, 128, 4, n).transpose(0, 1, 3, 2))
    if fmt == "e4m3":
        words = by_word.astype(ml_dtypes.float8_e4m3fn).view(np.uint8)
    else:
        c = by_word.astype(ml_dtypes.float4_e2m1fn).view(np.uint8) & 0xF
        words = (c[..., 0::2] | (c[..., 1::2] << 4)).reshape(k // 512, 128, 2 * n)
    return np.ascontiguousarray(words), np.ascontiguousarray(byte.astype(np.uint8).reshape(k // 512, 16, n))


def unpack_weight(words, scales, fmt):
    g, _, n = scales.shape
    words = np.ascontiguousarray(words).reshape(g, 128, n, -1)
    if fmt == "e4m3":
        vals = words.view(ml_dtypes.float8_e4m3fn).astype(np.float64)
    else:
        nib = np.empty((g, 128, n, 4), np.uint8)
        nib[..., 0::2] = words & 0xF
        nib[..., 1::2] = words >> 4
        vals = E2M1[nib]
    vals = vals * np.repeat(np.exp2(scales.astype(np.float64) - 127.0), 8, axis=1)[..., None]
    return vals.transpose(0, 1, 3, 2).reshape(g * 512, n)


def gelu(v):
    return 0.5 * v * (1.0 + np.tanh(np.sqrt(2.0 / np.pi) * (v + 0.044715 * v**3)))


def bf(x):
    return np.asarray(x, np.float32).astype(ml_dtypes.bfloat16)


def planes(Y):
    n, m = Y.shape
    b = f64(bf(Y)).reshape(n // 32, 32, m)
    amax = np.abs(b).max(1)
    byte = np.clip(np.where(amax > 0, np.frexp(amax)[1] - 1 + 127 - 7, 1), 1, 254)
    codes = (b * np.exp2(127.0 - byte)[:, None, :]).reshape(n, m).astype(np.float32).astype(ml_dtypes.float8_e4m3fn).view(np.uint8)
    words = codes.reshape(n // 512, 128, 4, m).transpose(0, 1, 3, 2)
    return np.ascontiguousarray(words), np.ascontiguousarray(byte.astype(np.uint8).reshape(n // 512, 16, m))


K, K2, H, N, T, S = 1024, 512, 1024, 512, 4096, 1024


def setup_inputs():
    n = np.random.standard_normal
    s = mx_kscale(K)[:, None]
    s2 = mx_kscale(K2)[:, None]
    u = mx_kscale(H)[:, None]
    d = {}
    d["tab_words"], d["tab_scales"] = pack_weight(n((K, T)) * s, "e4m3")
    d["offs"] = striped(np.random.permutation(T)[:S])
    d["xs_words"], d["xs_scales"] = pack_weight(n((K2, S)) * s2, "e4m3")
    d["w1"] = (0.38 * n((K, H)) / K ** 0.5 / s).astype(np.float32)
    d["w2_words"], d["w2_scales"] = pack_weight(0.32 * n((K2, H)) / K2 ** 0.5 / s2, "e2m1")
    d["phase"] = np.random.uniform(-0.5, 0.5, H).astype(np.float32)
    d["gain"] = (np.exp(0.3 * n(H)) * u[:, 0]).astype(np.float32)
    d["w3"] = (n((H, N)) / H ** 0.5 / u * np.exp(0.8 * n(N))[None, :]).astype(np.float32)
    return d


def reference(tab_words, tab_scales, offs, xs_words, xs_scales, w1, w2_words, w2_scales, phase, gain, w3):
    v = unpack_weight(tab_words, tab_scales, "e4m3")[:, unstriped(offs)]
    xs = unpack_weight(xs_words, xs_scales, "e4m3")
    w2 = unpack_weight(w2_words, w2_scales, "e2m1")
    a = mxq(f64(w1), 0, "e4m3").T @ v
    b = (w2.T @ xs) + f64(phase)[:, None]
    h = (np.sin(a + b) + a) * f64(gain)[:, None]
    y = mxq(f64(w3), 0, "e4m3").T @ mxq(h, 0, "e4m3")
    words, scales = planes(y)
    return y, words, scales

@@ -1,0 +1,274 @@
+import math
+from contextlib import ExitStack
+
+import concourse.mybir as mybir
+
+K, K2, H, N, T, S = 1024, 512, 1024, 512, 4096, 1024
+FLOPS = 2 * (K * H * S + K2 * H * S + H * N * S)
+
+F32 = mybir.dt.float32
+BF16 = mybir.dt.bfloat16
+I32 = mybir.dt.int32
+U32 = mybir.dt.uint32
+U16 = mybir.dt.uint16
+U8 = mybir.dt.uint8
+E4M3 = mybir.dt.float8_e4m3fn_x4
+E2M1 = mybir.dt.float4_e2m1fn_x4
+ALU = mybir.AluOpType
+ACT = mybir.ActivationFunctionType
+
+P = 128
+PACK = 4
+K_PASS = P * PACK
+CUES = 128
+HALF = 512
+TURN = 2.0 * math.pi
+ROUNDER = 1.5 * 2.0**23
+
+
+def tile_list_firing_script_scores_kernel(
+    tc, tab_words, tab_scales, offs, xs_words, xs_scales, w1, w2_words, w2_scales, phase, gain, w3, out_0, out_1, out_2
+):
+    nc = tc.nc
+    with ExitStack() as ctx:
+        keep = ctx.enter_context(tc.tile_pool(name="keep", bufs=1))
+        work = ctx.enter_context(tc.tile_pool(name="work", bufs=3))
+        psum = ctx.enter_context(tc.psum_pool(name="psum", bufs=1))
+
+        offsets = keep.tile([P, S // 16], U16, name="offsets")
+        table = [keep.tile([P, T], I32, name=f"table{a}", align_bytes=64) for a in range(2)]
+        table_scales = keep.tile([P, T], U8, name="table_scales", align_bytes=64)
+        xs_codes = keep.tile([P, S], I32, name="xs_codes", align_bytes=64)
+        xs_plane = keep.tile([P, S], U8, name="xs_plane", align_bytes=64)
+        w2_raw = keep.tile([P, 2 * H], U8, name="w2_raw", align_bytes=64)
+        w2_raw_plane = keep.tile([P, H], U8, name="w2_raw_plane", align_bytes=64)
+        phase_sb = keep.tile([P, 2, PACK], F32, name="phase_sb")
+        phase_turns = keep.tile([P, 2, PACK], F32, name="phase_turns")
+        gain_sb = keep.tile([P, 2, PACK], F32, name="gain_sb")
+        warm = keep.tile([P, 1], F32, name="warm")
+        warm_out = keep.tile([P, 1], F32, name="warm_out")
+
+        nc.gpsimd.memset(w2_raw_plane[:].bitcast(I32), 0)
+        nc.gpsimd.memset(xs_plane[:].bitcast(I32), 0)
+        nc.gpsimd.memset(table_scales[:].bitcast(I32), 0)
+        nc.vector.memset(warm[:], 0.0)
+        nc.scalar.activation(warm_out[:], warm[:], ACT.Sin)
+
+        def load_table(a, half):
+            cols = slice(half * T // 2, (half + 1) * T // 2)
+            nc.sync.dma_start(table[a][:, cols], tab_words[a].rearrange("p n t -> p (n t)").bitcast(I32)[:, cols])
+
+        nc.sync.dma_start(w2_raw[:].bitcast(I32), w2_words[0].bitcast(I32))
+        for q in range(4):
+            nc.sync.dma_start(w2_raw_plane[32 * q : 32 * q + 4, :].bitcast(I32), w2_scales[0, 4 * q : 4 * q + 4, :].bitcast(I32))
+        nc.sync.dma_start(xs_codes[:], xs_words[0].rearrange("p n t -> p (n t)").bitcast(I32))
+        nc.sync.dma_start(phase_sb[:], phase.rearrange("(b p t) -> p b t", p=P, t=PACK))
+        load_table(0, 0)
+        for q in range(4):
+            nc.sync.dma_start(xs_plane[32 * q : 32 * q + 4, :].bitcast(I32), xs_scales[0, 4 * q : 4 * q + 4, :].bitcast(I32))
+        load_table(0, 1)
+        nc.sync.dma_start(offsets[:], offs)
+        for q in range(4):
+            nc.sync.dma_start(table_scales[32 * q : 32 * q + 8, :].bitcast(I32), tab_scales[:, 4 * q : 4 * q + 4, :].bitcast(I32))
+        load_table(1, 0)
+        nc.sync.dma_start(gain_sb[:], gain.rearrange("(b p t) -> p b t", p=P, t=PACK))
+        load_table(1, 1)
+
+        raw = {}
+        for name, w, b, a in (("w1", w1, 0, 0), ("w1", w1, 0, 1), ("w1", w1, 1, 0), ("w1", w1, 1, 1), ("w3", w3, 0, 0), ("w3", w3, 0, 1)):
+            raw_tile = keep.tile([P, PACK, HALF], F32, name=f"{name}_raw{b}{a}")
+            rows = w[a * K_PASS : (a + 1) * K_PASS, b * HALF : (b + 1) * HALF]
+            nc.sync.dma_start(raw_tile[:], rows.rearrange("(p j) c -> p j c", j=PACK))
+            raw[name, b, a] = raw_tile
+
+        rounded, codes, planes = {}, {}, {}
+        for key in raw:
+            tag = "%s_%d%d" % key
+            codes[key] = keep.tile([P, HALF], U32, name="codes_" + tag, align_bytes=64)
+            planes[key] = keep.tile([P, HALF], U8, name="plane_" + tag, align_bytes=64)
+
+        def round_weight(key, engine, part, parts):
+            if part == 0:
+                rounded[key] = work.tile([P, PACK, P, PACK], BF16, name="rounded", tag="rounded", bufs=2, align_bytes=64)
+            m = slice(part * P // parts, (part + 1) * P // parts)
+            src = raw[key][:].rearrange("p j (m t) -> p m j t", t=PACK)[:, m]
+            dst = rounded[key][:].rearrange("p t m j -> p m j t")[:, m]
+            if engine == "vector":
+                nc.vector.tensor_copy(dst, src)
+            else:
+                nc.scalar.copy(dst, src)
+
+        def quantize_weight(key):
+            nc.vector.quantize_mx(
+                out=codes[key][:].bitcast(E4M3), scales=planes[key][:], in_=rounded[key][:].rearrange("p t m j -> p (t m j)")
+            )
+
+        nc.vector.tensor_scalar(phase_turns[:], phase_sb[:], 1.0 / TURN, None, ALU.mult)
+        bank_count = [0]
+
+        def next_bank(shape):
+            index = bank_count[0] % 5
+            bank_count[0] += 1
+            return psum.tile(shape, F32, name="bank", tag=f"bank{index}")
+
+        b_turns = {}
+        for b in range(2):
+            w2_codes = keep.tile([P, PACK, P, 2], U8, name=f"w2_codes{b}", align_bytes=64)
+            w2_plane = keep.tile([P, PACK, P], U8, name=f"w2_plane{b}", align_bytes=64)
+            nc.vector.tensor_copy(
+                w2_codes[:], w2_raw[:, 2 * HALF * b : 2 * HALF * (b + 1)].rearrange("p (m t e) -> p t m e", t=PACK, e=2)
+            )
+            nc.vector.tensor_copy(w2_plane[:], w2_raw_plane[:, HALF * b : HALF * (b + 1)].rearrange("p (m t) -> p t m", t=PACK))
+            for half in range(2):
+                cols = slice(half * HALF, (half + 1) * HALF)
+                b_turns[b, half] = keep.tile([P, PACK, HALF], F32, name=f"b_turns{b}{half}")
+                for t in range(PACK):
+                    bank = next_bank([P, HALF])
+                    nc.tensor.matmul_mx(
+                        out=bank[:],
+                        lhsT=w2_codes[:, t].rearrange("p m e -> p (m e)").bitcast(E2M1),
+                        lhsT_scale=w2_plane[:, t],
+                        rhs=xs_codes[:, cols].bitcast(E4M3),
+                        rhs_scale=xs_plane[:, cols],
+                        start=True,
+                        stop=True,
+                    )
+                    nc.scalar.activation(
+                        b_turns[b, half][:, t], bank[:], ACT.Identity, bias=phase_turns[:, b, t : t + 1], scale=1.0 / TURN
+                    )
+
+        picked_plane = keep.tile([P, S], U8, name="picked_plane", align_bytes=64)
+        picked = [keep.tile([P, S], I32, name=f"picked{a}", align_bytes=64) for a in range(2)]
+        for a in range(2):
+            if a == 1:
+                nc.vector.tensor_copy(picked_plane[:], table_scales[:].indirect(offsets[:]))
+            nc.vector.tensor_copy(picked[a][:].bitcast(U32), table[a][:].bitcast(U32).indirect(offsets[:]))
+        for a in range(2):
+            for part in range(2):
+                round_weight(("w1", 0, a), "vector", part, 2)
+            quantize_weight(("w1", 0, a))
+
+        chunks = S // CUES
+        units = [(b, c) for b in range(2) for c in range(chunks)]
+        a_bank, z, whole, frac, sine, summed, h_bf = {}, {}, {}, {}, {}, {}, {}
+        h_codes = [keep.tile([P, S], U32, name=f"h_codes{b}", align_bytes=64) for b in range(2)]
+        h_plane = [keep.tile([P, S], U8, name=f"h_plane{b}", align_bytes=64) for b in range(2)]
+        y_codes = keep.tile([P, S], I32, name="y_codes", align_bytes=64)
+        y_plane = keep.tile([P, S], U8, name="y_plane", align_bytes=64)
+        y_bank, y_bf = {}, {}
+        out_rows = out_0.rearrange("(p t) j -> p t j", t=PACK)
+        out_words = out_1[0].rearrange("p m t -> p (m t)").bitcast(I32)
+
+        def product_a(i):
+            b, c = units[i]
+            cols = slice(c * CUES, (c + 1) * CUES)
+            a_bank[i] = next_bank([P, PACK, CUES])
+            for t in range(PACK):
+                w_cols = slice(t * P, (t + 1) * P)
+                for a in range(2):
+                    nc.tensor.matmul_mx(
+                        out=a_bank[i][:, t],
+                        lhsT=codes["w1", b, a][:, w_cols].bitcast(E4M3),
+                        lhsT_scale=planes["w1", b, a][:, w_cols],
+                        rhs=picked[a][:, cols].bitcast(E4M3),
+                        rhs_scale=picked_plane[4 * a :, cols],
+                        start=(a == 0),
+                        stop=(a == 1),
+                    )
+
+        def angle(i):
+            b, c = units[i]
+            half, c0 = divmod(c * CUES, HALF)
+            z[i] = work.tile([P, PACK, CUES], F32, name="z", tag="z")
+            nc.vector.scalar_tensor_tensor(
+                z[i][:], a_bank[i][:], 1.0 / TURN, b_turns[b, half][:, :, c0 : c0 + CUES], ALU.mult, ALU.add
+            )
+            whole[i] = work.tile([P, PACK, CUES], U32, name="whole", tag="whole")
+            nc.scalar.activation(whole[i][:], z[i][:], ACT.Copy, bias=ROUNDER)
+
+        def reduce_angle(i):
+            frac[i] = work.tile([P, PACK, CUES], F32, name="frac", tag="frac")
+            nc.vector.scalar_tensor_tensor(frac[i][:], whole[i][:].bitcast(I32), ROUNDER, z[i][:], ALU.subtract, ALU.subtract)
+            sine[i] = work.tile([P, CUES, PACK], F32, name="sine", tag="sine")
+            nc.scalar.activation(
+                sine[i][:].rearrange("p (c i) t -> p c t i", i=PACK),
+                frac[i][:].rearrange("p t (c i) -> p c t i", i=PACK),
+                ACT.Sin,
+                scale=-TURN,
+            )
+
+        def add_residual(i):
+            summed[i] = work.tile([P, CUES, PACK], F32, name="summed", tag="summed")
+            nc.vector.tensor_tensor(summed[i][:], a_bank[i][:].rearrange("p t n -> p n t"), sine[i][:], ALU.add)
+
+        def apply_gain(i):
+            b, c = units[i]
+            h_bf[i] = work.tile([P, CUES, PACK], BF16, name="h_bf", tag="h_bf", align_bytes=64)
+            nc.vector.tensor_tensor(h_bf[i][:], summed[i][:], gain_sb[:, b].unsqueeze(1).to_broadcast([P, CUES, PACK]), ALU.mult)
+
+        def quantize_h(i):
+            b, c = units[i]
+            cols = slice(c * CUES, (c + 1) * CUES)
+            nc.vector.quantize_mx(
+                out=h_codes[b][:, cols].bitcast(E4M3), scales=h_plane[b][:, cols], in_=h_bf[i][:].rearrange("p n t -> p (n t)")
+            )
+
+        def product_y(c):
+            cols = slice(c * CUES, (c + 1) * CUES)
+            y_bank[c] = psum.tile([P, PACK, CUES], F32, name="y_bank", tag=f"y_bank{c % 3}")
+            for t in range(PACK):
+                w_cols = slice(t * P, (t + 1) * P)
+                for a in range(2):
+                    nc.tensor.matmul_mx(
+                        out=y_bank[c][:, t],
+                        lhsT=codes["w3", 0, a][:, w_cols].bitcast(E4M3),
+                        lhsT_scale=planes["w3", 0, a][:, w_cols],
+                        rhs=h_codes[a][:, cols].bitcast(E4M3),
+                        rhs_scale=h_plane[a][:, cols],
+                        start=(a == 0),
+                        stop=(a == 1),
+                    )
+            y_bf[c] = work.tile([P, CUES, PACK], BF16, name="y_bf", tag="y_bf", align_bytes=64)
+            nc.scalar.copy(y_bf[c][:], y_bank[c][:].rearrange("p t n -> p n t"))
+            y_sb = work.tile([P, PACK, CUES], F32, name="y_sb", tag="y_sb")
+            nc.scalar.copy(y_sb[:], y_bank[c][:])
+            nc.sync.dma_start(out_rows[:, :, cols], y_sb[:])
+
+        def quantize_y(c):
+            cols = slice(c * CUES, (c + 1) * CUES)
+            nc.vector.quantize_mx(
+                out=y_codes[:, cols].bitcast(E4M3), scales=y_plane[:, cols], in_=y_bf[c][:].rearrange("p n t -> p (n t)")
+            )
+            if c % 2 == 1:
+                pair = slice((c - 1) * CUES, (c + 1) * CUES)
+                nc.sync.dma_start(out_words[:, pair], y_codes[:, pair])
+
+        later = [("w1", 1, 0), ("w1", 1, 1), ("w3", 0, 0), ("w3", 0, 1)]
+        parts = 4
+        n = len(units)
+        product_a(0)
+        for step in range(n + 7):
+            if step + 1 < n:
+                product_a(step + 1)
+            if step < n:
+                angle(step)
+            if 0 <= step - 1 < n:
+                reduce_angle(step - 1)
+            if 0 <= step - 2 < n:
+                add_residual(step - 2)
+            if 0 <= step - 3 < n:
+                apply_gain(step - 3)
+            if 0 <= step - 4 < n:
+                quantize_h(step - 4)
+                if step - 4 >= chunks:
+                    product_y(step - 4 - chunks)
+            if 0 <= step - 5 - chunks < chunks:
+                quantize_y(step - 5 - chunks)
+            if 1 <= step <= 2 * len(later):
+                key = later[(step - 1) // 2]
+                for part in range(2):
+                    round_weight(key, "scalar", 2 * ((step - 1) % 2) + part, parts)
+            if 3 <= step <= 2 * len(later) + 1 and step % 2 == 1:
+                quantize_weight(later[(step - 3) // 2])
+        for q in range(4):
+            nc.sync.dma_start(out_2[0, 4 * q : 4 * q + 4, :].bitcast(I32), y_plane[32 * q : 32 * q + 4, :].bitcast(I32))

@@ -2,6 +2,7 @@ import math
 from contextlib import ExitStack
 
 import concourse.mybir as mybir
+from concourse.masks import make_identity
 
 K, K2, H, N, T, S = 1024, 512, 1024, 512, 4096, 1024
 FLOPS = 2 * (K * H * S + K2 * H * S + H * N * S)
@@ -23,7 +24,12 @@ K_PASS = P * PACK
 CUES = 128
 HALF = 512
 TURN = 2.0 * math.pi
-ROUNDER = 1.5 * 2.0**23
+LEAD = 5
+LAG = 4
+FIRST_B = 12
+COPY_A_FROM = 12
+ROUND_ON_VECTOR_FROM = 5
+GAIN_ON_SCALAR = range(2, 7)
 
 
 def tile_list_firing_script_scores_kernel(
@@ -36,175 +42,276 @@ def tile_list_firing_script_scores_kernel(
         psum = ctx.enter_context(tc.psum_pool(name="psum", bufs=1))
 
         offsets = keep.tile([P, S // 16], U16, name="offsets")
-        table = [keep.tile([P, T], I32, name=f"table{a}", align_bytes=64) for a in range(2)]
+        table = [keep.tile([P, T], I32, name=f"table{a}", tag=f"table{a}", align_bytes=64) for a in range(2)]
         table_scales = keep.tile([P, T], U8, name="table_scales", align_bytes=64)
         xs_codes = keep.tile([P, S], I32, name="xs_codes", align_bytes=64)
         xs_plane = keep.tile([P, S], U8, name="xs_plane", align_bytes=64)
-        w2_raw = keep.tile([P, 2 * H], U8, name="w2_raw", align_bytes=64)
-        w2_raw_plane = keep.tile([P, H], U8, name="w2_raw_plane", align_bytes=64)
-        phase_sb = keep.tile([P, 2, PACK], F32, name="phase_sb")
-        phase_turns = keep.tile([P, 2, PACK], F32, name="phase_turns")
+        w2_codes = keep.tile([P, 2 * H], U8, name="w2_codes", align_bytes=64)
+        w2_plane = keep.tile([P, H], U8, name="w2_plane", align_bytes=64)
+        phase_dealt = keep.tile([P, 2, PACK], F32, name="phase_dealt")
+        phase_rows = keep.tile([P, PACK], F32, name="phase_rows")
         gain_sb = keep.tile([P, 2, PACK], F32, name="gain_sb")
+        identity = keep.tile([P, P], F32, name="identity")
         warm = keep.tile([P, 1], F32, name="warm")
         warm_out = keep.tile([P, 1], F32, name="warm_out")
 
-        nc.gpsimd.memset(w2_raw_plane[:].bitcast(I32), 0)
+        nc.gpsimd.memset(w2_plane[:].bitcast(I32), 0)
         nc.gpsimd.memset(xs_plane[:].bitcast(I32), 0)
-        nc.gpsimd.memset(table_scales[:].bitcast(I32), 0)
         nc.vector.memset(warm[:], 0.0)
+        nc.vector.memset(table_scales[:].bitcast(I32), 0)
+        make_identity(nc, identity[:])
         nc.scalar.activation(warm_out[:], warm[:], ACT.Sin)
+
+        raw = {}
 
         def load_table(a, half):
             cols = slice(half * T // 2, (half + 1) * T // 2)
             nc.sync.dma_start(table[a][:, cols], tab_words[a].rearrange("p n t -> p (n t)").bitcast(I32)[:, cols])
 
-        nc.sync.dma_start(w2_raw[:].bitcast(I32), w2_words[0].bitcast(I32))
-        for q in range(4):
-            nc.sync.dma_start(w2_raw_plane[32 * q : 32 * q + 4, :].bitcast(I32), w2_scales[0, 4 * q : 4 * q + 4, :].bitcast(I32))
-        nc.sync.dma_start(xs_codes[:], xs_words[0].rearrange("p n t -> p (n t)").bitcast(I32))
-        nc.sync.dma_start(phase_sb[:], phase.rearrange("(b p t) -> p b t", p=P, t=PACK))
-        load_table(0, 0)
-        for q in range(4):
+        def load_weight(name, w, b, a, pieces=1):
+            width = HALF // pieces
+            rows = w[a * K_PASS : (a + 1) * K_PASS, b * HALF : (b + 1) * HALF].rearrange("(p j) c -> p j c", j=PACK)
+            for piece in range(pieces):
+                tile = keep.tile([P, PACK, width], F32, name=f"{name}_raw{b}{a}{piece}")
+                nc.sync.dma_start(tile[:], rows[:, :, piece * width : (piece + 1) * width])
+                for half in range(piece, 2, pieces):
+                    raw[name, b, a, half] = tile[:] if name == "w3" or pieces == 2 else tile[:, :, half * HALF // 2 : (half + 1) * HALF // 2]
+
+        def load_stream_scales(q):
+            nc.sync.dma_start(w2_plane[32 * q : 32 * q + 4, :].bitcast(I32), w2_scales[0, 4 * q : 4 * q + 4, :].bitcast(I32))
             nc.sync.dma_start(xs_plane[32 * q : 32 * q + 4, :].bitcast(I32), xs_scales[0, 4 * q : 4 * q + 4, :].bitcast(I32))
-        load_table(0, 1)
+
+        nc.sync.dma_start(phase_dealt[:], phase.rearrange("(b p t) -> p b t", p=P, t=PACK))
+        load_stream_scales(0)
+        nc.sync.dma_start(w2_codes[:].bitcast(I32), w2_words[0].bitcast(I32))
+        nc.sync.dma_start(xs_codes[:], xs_words[0].rearrange("p n t -> p (n t)").bitcast(I32))
+        for q in range(1, 4):
+            load_stream_scales(q)
+        load_table(0, 0)
         nc.sync.dma_start(offsets[:], offs)
+        load_table(0, 1)
         for q in range(4):
             nc.sync.dma_start(table_scales[32 * q : 32 * q + 8, :].bitcast(I32), tab_scales[:, 4 * q : 4 * q + 4, :].bitcast(I32))
         load_table(1, 0)
-        nc.sync.dma_start(gain_sb[:], gain.rearrange("(b p t) -> p b t", p=P, t=PACK))
         load_table(1, 1)
-
-        raw = {}
-        for name, w, b, a in (("w1", w1, 0, 0), ("w1", w1, 0, 1), ("w1", w1, 1, 0), ("w1", w1, 1, 1), ("w3", w3, 0, 0), ("w3", w3, 0, 1)):
-            raw_tile = keep.tile([P, PACK, HALF], F32, name=f"{name}_raw{b}{a}")
-            rows = w[a * K_PASS : (a + 1) * K_PASS, b * HALF : (b + 1) * HALF]
-            nc.sync.dma_start(raw_tile[:], rows.rearrange("(p j) c -> p j c", j=PACK))
-            raw[name, b, a] = raw_tile
+        load_weight("w1", w1, 0, 0, pieces=2)
+        nc.sync.dma_start(gain_sb[:], gain.rearrange("(b p t) -> p b t", p=P, t=PACK))
+        load_weight("w1", w1, 0, 1, pieces=2)
+        for a in range(2):
+            load_weight("w1", w1, 1, a)
+        for a in range(2):
+            load_weight("w3", w3, 0, a)
 
         rounded, codes, planes = {}, {}, {}
-        for key in raw:
-            tag = "%s_%d%d" % key
-            codes[key] = keep.tile([P, HALF], U32, name="codes_" + tag, align_bytes=64)
-            planes[key] = keep.tile([P, HALF], U8, name="plane_" + tag, align_bytes=64)
+        later = [(name, b, a, half) for name, b in (("w1", 1), ("w3", 0)) for a in range(2) for half in range(2)]
+        joint = keep.tile([P, HALF * PACK], BF16, name="joint", align_bytes=64)
+        for half in range(2):
+            rounded[later[half]] = joint[:, half * 2 * HALF : (half + 1) * 2 * HALF].rearrange("p (c j) -> p c j", j=PACK)
+        rounded["w1", 0, 0, 0] = rounded[later[0]]
+        for name, b, a in sorted({key[:3] for key in raw}):
+            codes[name, b, a] = keep.tile([P, HALF], U32, name=f"codes_{name}{b}{a}", align_bytes=64)
+            planes[name, b, a] = keep.tile([P, HALF], U8, name=f"plane_{name}{b}{a}", align_bytes=64)
 
-        def round_weight(key, engine, part, parts):
-            if part == 0:
-                rounded[key] = work.tile([P, PACK, P, PACK], BF16, name="rounded", tag="rounded", bufs=2, align_bytes=64)
-            m = slice(part * P // parts, (part + 1) * P // parts)
-            src = raw[key][:].rearrange("p j (m t) -> p m j t", t=PACK)[:, m]
-            dst = rounded[key][:].rearrange("p t m j -> p m j t")[:, m]
-            if engine == "vector":
-                nc.vector.tensor_copy(dst, src)
+        def round_weight(key, tag, copy=nc.scalar.copy):
+            if key not in rounded:
+                rounded[key] = work.tile([P, HALF // 2, PACK], BF16, name="rounded", tag=tag, bufs=1, align_bytes=64)
+            src = raw[key].rearrange("p j (m t) -> p m j t", t=PACK)
+            if key[0] == "w3":
+                src = src[:, :, :, 2 * key[3] : 2 * key[3] + 2]
+                dst = rounded[key][:].rearrange("p (t m) j -> p m j t", t=2)
             else:
-                nc.scalar.copy(dst, src)
+                dst = rounded[key][:].rearrange("p (m t) j -> p m j t", t=PACK)
+            copy(dst, src)
 
         def quantize_weight(key):
+            cols = slice(key[3] * HALF // 2, (key[3] + 1) * HALF // 2)
+            if key == later[0]:
+                return
+            if key == later[1]:
+                nc.vector.quantize_mx(
+                    out=codes[key[:3]][:].bitcast(E4M3), scales=planes[key[:3]][:], in_=joint[:]
+                )
+                return
             nc.vector.quantize_mx(
-                out=codes[key][:].bitcast(E4M3), scales=planes[key][:], in_=rounded[key][:].rearrange("p t m j -> p (t m j)")
+                out=codes[key[:3]][:, cols].bitcast(E4M3),
+                scales=planes[key[:3]][:, cols],
+                in_=rounded[key][:].rearrange("p c j -> p (c j)"),
             )
 
-        nc.vector.tensor_scalar(phase_turns[:], phase_sb[:], 1.0 / TURN, None, ALU.mult)
-        bank_count = [0]
+        def bank(kind, index):
+            return psum.tile([P, HALF], F32, name="bank", tag=f"{kind}{index}")
 
-        def next_bank(shape):
-            index = bank_count[0] % 5
-            bank_count[0] += 1
-            return psum.tile(shape, F32, name="bank", tag=f"bank{index}")
+        chunks = S // CUES
+        units = [(0, c) for c in range(LEAD)]
+        behind = 0
+        for c in range(LEAD, chunks + 1):
+            catch_up = min(behind + 2, c)
+            units.extend((1, k) for k in range(behind, catch_up))
+            behind = catch_up
+            if c < chunks:
+                units.append((0, c))
+        n = len(units)
 
-        b_turns = {}
+        minus_phase = keep.tile([P, 2, HALF], F32, name="minus_phase")
+        spread = [bank("y", b) for b in range(2)]
         for b in range(2):
-            w2_codes = keep.tile([P, PACK, P, 2], U8, name=f"w2_codes{b}", align_bytes=64)
-            w2_plane = keep.tile([P, PACK, P], U8, name=f"w2_plane{b}", align_bytes=64)
-            nc.vector.tensor_copy(
-                w2_codes[:], w2_raw[:, 2 * HALF * b : 2 * HALF * (b + 1)].rearrange("p (m t e) -> p t m e", t=PACK, e=2)
-            )
-            nc.vector.tensor_copy(w2_plane[:], w2_raw_plane[:, HALF * b : HALF * (b + 1)].rearrange("p (m t) -> p t m", t=PACK))
-            for half in range(2):
-                cols = slice(half * HALF, (half + 1) * HALF)
-                b_turns[b, half] = keep.tile([P, PACK, HALF], F32, name=f"b_turns{b}{half}")
-                for t in range(PACK):
-                    bank = next_bank([P, HALF])
-                    nc.tensor.matmul_mx(
-                        out=bank[:],
-                        lhsT=w2_codes[:, t].rearrange("p m e -> p (m e)").bitcast(E2M1),
-                        lhsT_scale=w2_plane[:, t],
-                        rhs=xs_codes[:, cols].bitcast(E4M3),
-                        rhs_scale=xs_plane[:, cols],
-                        start=True,
-                        stop=True,
-                    )
-                    nc.scalar.activation(
-                        b_turns[b, half][:, t], bank[:], ACT.Identity, bias=phase_turns[:, b, t : t + 1], scale=1.0 / TURN
-                    )
+            for t in range(PACK):
+                nc.tensor.transpose(spread[b][:, t * P : (t + 1) * P], phase_dealt[:, b, t : t + 1].to_broadcast([P, P]), identity[:])
+            nc.scalar.activation(minus_phase[:, b], spread[b][:], ACT.Copy, scale=-1.0)
 
         picked_plane = keep.tile([P, S], U8, name="picked_plane", align_bytes=64)
         picked = [keep.tile([P, S], I32, name=f"picked{a}", align_bytes=64) for a in range(2)]
-        for a in range(2):
-            if a == 1:
-                nc.vector.tensor_copy(picked_plane[:], table_scales[:].indirect(offsets[:]))
-            nc.vector.tensor_copy(picked[a][:].bitcast(U32), table[a][:].bitcast(U32).indirect(offsets[:]))
-        for a in range(2):
-            for part in range(2):
-                round_weight(("w1", 0, a), "vector", part, 2)
-            quantize_weight(("w1", 0, a))
 
-        chunks = S // CUES
-        units = [(b, c) for b in range(2) for c in range(chunks)]
-        a_bank, z, whole, frac, sine, summed, h_bf = {}, {}, {}, {}, {}, {}, {}
+        minus_b = {}
+        for i in range(n):
+            minus_b[units[i]] = keep.tile([P, PACK, P], F32, name=f"minus_b{i}")
+        on_vector = [u for u in units if u[0] == 0 or u[1] < PACK]
+
+        def subtract_b(i):
+            b, c = on_vector[i]
+            cols = slice(c * CUES, (c + 1) * CUES)
+            b_bank = bank("a", i % 3)
+            nc.tensor.matmul_mx(
+                out=b_bank[:],
+                lhsT=xs_codes[:, cols].bitcast(E4M3),
+                lhsT_scale=xs_plane[:, cols],
+                rhs=w2_codes[:, 2 * HALF * b : 2 * HALF * (b + 1)].bitcast(E2M1),
+                rhs_scale=w2_plane[:, HALF * b : HALF * (b + 1)],
+                start=True,
+                stop=True,
+            )
+            nc.vector.tensor_tensor(
+                minus_b[b, c][:],
+                minus_phase[:, b].rearrange("p (t m) -> p t m", t=PACK),
+                b_bank[:].rearrange("p (m t) -> p t m", t=PACK),
+                ALU.subtract,
+            )
+
+        for i in range(FIRST_B):
+            subtract_b(i)
+        phase_row = work.tile([P, P, PACK], F32, name="phase_row", tag="staged3", bufs=1, align_bytes=64)
+        nc.scalar.copy(phase_row[:], spread[1][:].rearrange("p (t m) -> p m t", t=PACK))
+        turned = bank("h", 2)
+        for g in range(PACK):
+            nc.tensor.transpose(turned[:, g * P : (g + 1) * P], phase_row[:].rearrange("p m t -> p (m t)")[:, g * P : (g + 1) * P], identity[:])
+        nc.scalar.copy(phase_rows[:], turned[:].rearrange("p (g m) -> p g m", g=PACK)[:, :, 0])
+
+        nc.vector.tensor_copy(picked[0][:].bitcast(U32), table[0][:].bitcast(U32).indirect(offsets[:]))
+        nc.vector.tensor_copy(picked_plane[:], table_scales[:].indirect(offsets[:]))
+        nc.vector.tensor_copy(picked[1][:].bitcast(U32), table[1][:].bitcast(U32).indirect(offsets[:]))
+        for half in range(1, 2):
+            cols = slice(half * HALF, (half + 1) * HALF)
+            by_channel = {}
+            for g in range(PACK):
+                first = HALF + g * P
+                b_bank = bank("y", (g + 1) % 2)
+                nc.tensor.matmul_mx(
+                    out=b_bank[:],
+                    lhsT=w2_codes[:, 2 * first : 2 * (first + P)].bitcast(E2M1),
+                    lhsT_scale=w2_plane[:, first : first + P],
+                    rhs=xs_codes[:, cols].bitcast(E4M3),
+                    rhs_scale=xs_plane[:, cols],
+                    start=True,
+                    stop=True,
+                )
+                if g == 0:
+                    by_channel[g] = joint[:, : 2 * HALF].bitcast(F32)
+                else:
+                    by_channel[g] = work.tile([P, HALF], F32, name="by_channel", tag=f"staged{g}", bufs=1, align_bytes=64)
+                nc.scalar.activation(by_channel[g][:], b_bank[:], ACT.Identity, bias=phase_rows[:, g : g + 1])
+            for k in range(PACK):
+                turned = bank("h", (half * PACK + k) % 3)
+                for g in range(PACK):
+                    nc.tensor.transpose(turned[:, g * P : (g + 1) * P], by_channel[g][:, k * CUES : (k + 1) * CUES], identity[:])
+                nc.scalar.activation(
+                    minus_b[1, half * PACK + k][:], turned[:].rearrange("p (m t) -> p t m", t=PACK), ACT.Copy, scale=-1.0
+                )
+
+        rounded["w1", 0, 1, 1] = keep.tile([P, HALF // 2, PACK], BF16, name="rounded_last", tag="table1", align_bytes=64)
+        for a in range(2):
+            for half in range(2):
+                round_weight(("w1", 0, a, half), f"staged{2 * a + half}", nc.vector.tensor_copy if (a, half) == (1, 1) else nc.scalar.copy)
+                quantize_weight(("w1", 0, a, half))
+
+        for i in range(FIRST_B, len(on_vector)):
+            subtract_b(i)
+
+        a_bank, z, whole, frac, sine, h_bank, h_bf = {}, {}, {}, {}, {}, {}, {}
         h_codes = [keep.tile([P, S], U32, name=f"h_codes{b}", align_bytes=64) for b in range(2)]
         h_plane = [keep.tile([P, S], U8, name=f"h_plane{b}", align_bytes=64) for b in range(2)]
         y_codes = keep.tile([P, S], I32, name="y_codes", align_bytes=64)
         y_plane = keep.tile([P, S], U8, name="y_plane", align_bytes=64)
-        y_bank, y_bf = {}, {}
+        y_bf, y_sb, a_sb = {}, {}, {}
         out_rows = out_0.rearrange("(p t) j -> p t j", t=PACK)
         out_words = out_1[0].rearrange("p m t -> p (m t)").bitcast(I32)
 
         def product_a(i):
             b, c = units[i]
             cols = slice(c * CUES, (c + 1) * CUES)
-            a_bank[i] = next_bank([P, PACK, CUES])
-            for t in range(PACK):
-                w_cols = slice(t * P, (t + 1) * P)
-                for a in range(2):
-                    nc.tensor.matmul_mx(
-                        out=a_bank[i][:, t],
-                        lhsT=codes["w1", b, a][:, w_cols].bitcast(E4M3),
-                        lhsT_scale=planes["w1", b, a][:, w_cols],
-                        rhs=picked[a][:, cols].bitcast(E4M3),
-                        rhs_scale=picked_plane[4 * a :, cols],
-                        start=(a == 0),
-                        stop=(a == 1),
-                    )
+            a_bank[i] = bank("a", i % 3)
+            for a in range(2):
+                nc.tensor.matmul_mx(
+                    out=a_bank[i][:],
+                    lhsT=picked[a][:, cols].bitcast(E4M3),
+                    lhsT_scale=picked_plane[4 * a :, cols],
+                    rhs=codes["w1", b, a][:].bitcast(E4M3),
+                    rhs_scale=planes["w1", b, a][:],
+                    start=(a == 0),
+                    stop=(a == 1),
+                )
 
         def angle(i):
-            b, c = units[i]
-            half, c0 = divmod(c * CUES, HALF)
-            z[i] = work.tile([P, PACK, CUES], F32, name="z", tag="z")
-            nc.vector.scalar_tensor_tensor(
-                z[i][:], a_bank[i][:], 1.0 / TURN, b_turns[b, half][:, :, c0 : c0 + CUES], ALU.mult, ALU.add
-            )
-            whole[i] = work.tile([P, PACK, CUES], U32, name="whole", tag="whole")
-            nc.scalar.activation(whole[i][:], z[i][:], ACT.Copy, bias=ROUNDER)
+            z[i] = work.tile([P, PACK, P], F32, name="z", tag="z", bufs=5)
+            dealt = a_bank[i][:].rearrange("p (m t) -> p t m", t=PACK)
+            nc.vector.tensor_tensor(z[i][:], dealt, minus_b[units[i]][:], ALU.subtract)
+            if i >= COPY_A_FROM:
+                a_sb[i] = work.tile([P, PACK, P], F32, name="a_sb", tag="a_sb", bufs=3)
+                nc.scalar.copy(a_sb[i][:], dealt)
+
+        def count_turns(i):
+            if i == 0:
+                whole[i] = joint[:, 2 * HALF :].bitcast(I32)
+            elif i < len(later) - 1:
+                whole[i] = work.tile([P, HALF], I32, name="whole", tag=f"early{i}", bufs=1, align_bytes=64)
+            else:
+                whole[i] = work.tile([P, HALF], I32, name="whole", tag="whole", bufs=2)
+            nc.vector.tensor_scalar(whole[i][:], z[i][:].rearrange("p t m -> p (t m)"), 1.0 / TURN, None, ALU.mult)
 
         def reduce_angle(i):
-            frac[i] = work.tile([P, PACK, CUES], F32, name="frac", tag="frac")
-            nc.vector.scalar_tensor_tensor(frac[i][:], whole[i][:].bitcast(I32), ROUNDER, z[i][:], ALU.subtract, ALU.subtract)
-            sine[i] = work.tile([P, CUES, PACK], F32, name="sine", tag="sine")
-            nc.scalar.activation(
-                sine[i][:].rearrange("p (c i) t -> p c t i", i=PACK),
-                frac[i][:].rearrange("p t (c i) -> p c t i", i=PACK),
-                ACT.Sin,
-                scale=-TURN,
+            frac[i] = work.tile([P, HALF], F32, name="frac", tag="frac")
+            sine[i] = work.tile([P, PACK, P], F32, name="sine", tag="sine")
+            nc.vector.scalar_tensor_tensor(
+                frac[i][:], z[i][:].rearrange("p t m -> p (t m)"), 1.0 / TURN, whole[i][:], ALU.mult, ALU.subtract
             )
+            nc.scalar.activation(sine[i][:].rearrange("p t m -> p (t m)"), frac[i][:], ACT.Sin, scale=TURN)
 
-        def add_residual(i):
-            summed[i] = work.tile([P, CUES, PACK], F32, name="summed", tag="summed")
-            nc.vector.tensor_tensor(summed[i][:], a_bank[i][:].rearrange("p t n -> p n t"), sine[i][:], ALU.add)
+        def turn_and_add(i):
+            h_bank[i] = bank("h", i % 3)
+            terms = (sine[i], a_sb[i]) if i >= COPY_A_FROM else (sine[i], z[i], minus_b[units[i]])
+            for number, term in enumerate(terms):
+                for t in range(PACK):
+                    nc.tensor.matmul(
+                        h_bank[i][:, t * P : (t + 1) * P],
+                        term[:, t],
+                        identity[:],
+                        start=(number == 0 and t == 0),
+                        stop=(number == len(terms) - 1 and t == PACK - 1),
+                        is_transpose=True,
+                    )
 
         def apply_gain(i):
             b, c = units[i]
             h_bf[i] = work.tile([P, CUES, PACK], BF16, name="h_bf", tag="h_bf", align_bytes=64)
-            nc.vector.tensor_tensor(h_bf[i][:], summed[i][:], gain_sb[:, b].unsqueeze(1).to_broadcast([P, CUES, PACK]), ALU.mult)
+            if i in GAIN_ON_SCALAR:
+                by_slot = work.tile([P, PACK, CUES], BF16, name="by_slot", tag="by_slot", bufs=2)
+                for t in range(PACK):
+                    nc.scalar.activation(by_slot[:, t], h_bank[i][:, t * P : (t + 1) * P], ACT.Copy, scale=gain_sb[:, b, t : t + 1])
+                nc.scalar.copy(
+                    h_bf[i][:].rearrange("p (n i) t -> p n t i", i=PACK), by_slot[:].rearrange("p t (n i) -> p n t i", i=PACK)
+                )
+            else:
+                gains = gain_sb[:, b].unsqueeze(1).to_broadcast([P, CUES, PACK])
+                nc.vector.tensor_tensor(h_bf[i][:], h_bank[i][:].rearrange("p (t n) -> p n t", t=PACK), gains, ALU.mult)
 
         def quantize_h(i):
             b, c = units[i]
@@ -215,24 +322,30 @@ def tile_list_firing_script_scores_kernel(
 
         def product_y(c):
             cols = slice(c * CUES, (c + 1) * CUES)
-            y_bank[c] = psum.tile([P, PACK, CUES], F32, name="y_bank", tag=f"y_bank{c % 3}")
-            for t in range(PACK):
-                w_cols = slice(t * P, (t + 1) * P)
-                for a in range(2):
+            y_bank = bank("y", c % 2)
+            for a in range(2):
+                for t in range(PACK):
+                    w_cols = slice(t * P, (t + 1) * P)
                     nc.tensor.matmul_mx(
-                        out=y_bank[c][:, t],
+                        out=y_bank[:, w_cols],
                         lhsT=codes["w3", 0, a][:, w_cols].bitcast(E4M3),
                         lhsT_scale=planes["w3", 0, a][:, w_cols],
                         rhs=h_codes[a][:, cols].bitcast(E4M3),
                         rhs_scale=h_plane[a][:, cols],
-                        start=(a == 0),
-                        stop=(a == 1),
+                        start=(a == 0 and t == 0),
+                        stop=(a == 1 and t == PACK - 1),
                     )
             y_bf[c] = work.tile([P, CUES, PACK], BF16, name="y_bf", tag="y_bf", align_bytes=64)
-            nc.scalar.copy(y_bf[c][:], y_bank[c][:].rearrange("p t n -> p n t"))
-            y_sb = work.tile([P, PACK, CUES], F32, name="y_sb", tag="y_sb")
-            nc.scalar.copy(y_sb[:], y_bank[c][:])
-            nc.sync.dma_start(out_rows[:, :, cols], y_sb[:])
+            if c < ROUND_ON_VECTOR_FROM:
+                nc.scalar.copy(y_bf[c][:], y_bank[:].rearrange("p (t n) -> p n t", t=PACK))
+            y_sb[c] = work.tile([P, PACK, CUES], F32, name="y_sb", tag="y_sb")
+            nc.scalar.copy(y_sb[c][:].rearrange("p t n -> p (t n)"), y_bank[:])
+            nc.sync.dma_start(out_rows[:, :, cols], y_sb[c][:])
+
+        def round_y(c):
+            nc.vector.tensor_copy(
+                y_bf[c][:].rearrange("p (n i) t -> p n t i", i=PACK), y_sb[c][:].rearrange("p t (n i) -> p n t i", i=PACK)
+            )
 
         def quantize_y(c):
             cols = slice(c * CUES, (c + 1) * CUES)
@@ -243,32 +356,34 @@ def tile_list_firing_script_scores_kernel(
                 pair = slice((c - 1) * CUES, (c + 1) * CUES)
                 nc.sync.dma_start(out_words[:, pair], y_codes[:, pair])
 
-        later = [("w1", 1, 0), ("w1", 1, 1), ("w3", 0, 0), ("w3", 0, 1)]
-        parts = 4
-        n = len(units)
         product_a(0)
-        for step in range(n + 7):
+        for step in range(n + 8):
+            if 2 <= step <= len(later):
+                quantize_weight(later[step - 1])
             if step + 1 < n:
                 product_a(step + 1)
             if step < n:
                 angle(step)
+            if 0 <= step - LAG - 1 < n:
+                quantize_h(step - LAG - 1)
+                if units[step - LAG - 1][0] == 1:
+                    product_y(units[step - LAG - 1][1])
+            if 0 <= step - LAG - 2 < n and units[step - LAG - 2][0] == 1 and units[step - LAG - 2][1] >= ROUND_ON_VECTOR_FROM:
+                round_y(units[step - LAG - 2][1])
+            if 0 <= step - LAG - 3 < n and units[step - LAG - 3][0] == 1:
+                quantize_y(units[step - LAG - 3][1])
             if 0 <= step - 1 < n:
                 reduce_angle(step - 1)
+            if step == 1:
+                round_weight(later[0], None)
+            if 1 <= step < len(later):
+                round_weight(later[step], f"early{step - 1}")
             if 0 <= step - 2 < n:
-                add_residual(step - 2)
-            if 0 <= step - 3 < n:
-                apply_gain(step - 3)
-            if 0 <= step - 4 < n:
-                quantize_h(step - 4)
-                if step - 4 >= chunks:
-                    product_y(step - 4 - chunks)
-            if 0 <= step - 5 - chunks < chunks:
-                quantize_y(step - 5 - chunks)
-            if 1 <= step <= 2 * len(later):
-                key = later[(step - 1) // 2]
-                for part in range(2):
-                    round_weight(key, "scalar", 2 * ((step - 1) % 2) + part, parts)
-            if 3 <= step <= 2 * len(later) + 1 and step % 2 == 1:
-                quantize_weight(later[(step - 3) // 2])
+                turn_and_add(step - 2)
+            if 0 <= step - LAG < n:
+                apply_gain(step - LAG)
+            if step < n:
+                count_turns(step)
         for q in range(4):
-            nc.sync.dma_start(out_2[0, 4 * q : 4 * q + 4, :].bitcast(I32), y_plane[32 * q : 32 * q + 4, :].bitcast(I32))
+            queue = nc.sync if q % 2 == 0 else nc.scalar
+            queue.dma_start(out_2[0, 4 * q : 4 * q + 4, :].bitcast(I32), y_plane[32 * q : 32 * q + 4, :].bitcast(I32))

import math
from contextlib import ExitStack

import concourse.mybir as mybir
from concourse.masks import make_identity

K, K2, H, N, T, S = 1024, 512, 1024, 512, 4096, 1024
FLOPS = 2 * (K * H * S + K2 * H * S + H * N * S)

F32 = mybir.dt.float32
BF16 = mybir.dt.bfloat16
I32 = mybir.dt.int32
U32 = mybir.dt.uint32
U16 = mybir.dt.uint16
U8 = mybir.dt.uint8
E4M3 = mybir.dt.float8_e4m3fn_x4
E2M1 = mybir.dt.float4_e2m1fn_x4
ALU = mybir.AluOpType
ACT = mybir.ActivationFunctionType

P = 128
PACK = 4
K_PASS = P * PACK
CUES = 128
HALF = 512
TURN = 2.0 * math.pi
LEAD = 5
LAG = 4
FIRST_B = 12
COPY_A_FROM = 12
ROUND_ON_VECTOR_FROM = 5
GAIN_ON_SCALAR = range(2, 7)


def tile_list_firing_script_scores_kernel(
    tc, tab_words, tab_scales, offs, xs_words, xs_scales, w1, w2_words, w2_scales, phase, gain, w3, out_0, out_1, out_2
):
    nc = tc.nc
    with ExitStack() as ctx:
        keep = ctx.enter_context(tc.tile_pool(name="keep", bufs=1))
        work = ctx.enter_context(tc.tile_pool(name="work", bufs=3))
        psum = ctx.enter_context(tc.psum_pool(name="psum", bufs=1))

        offsets = keep.tile([P, S // 16], U16, name="offsets")
        table = [keep.tile([P, T], I32, name=f"table{a}", tag=f"table{a}", align_bytes=64) for a in range(2)]
        table_scales = keep.tile([P, T], U8, name="table_scales", align_bytes=64)
        xs_codes = keep.tile([P, S], I32, name="xs_codes", align_bytes=64)
        xs_plane = keep.tile([P, S], U8, name="xs_plane", align_bytes=64)
        w2_codes = keep.tile([P, 2 * H], U8, name="w2_codes", align_bytes=64)
        w2_plane = keep.tile([P, H], U8, name="w2_plane", align_bytes=64)
        phase_dealt = keep.tile([P, 2, PACK], F32, name="phase_dealt")
        phase_rows = keep.tile([P, PACK], F32, name="phase_rows")
        gain_sb = keep.tile([P, 2, PACK], F32, name="gain_sb")
        identity = keep.tile([P, P], F32, name="identity")
        warm = keep.tile([P, 1], F32, name="warm")
        warm_out = keep.tile([P, 1], F32, name="warm_out")

        nc.gpsimd.memset(w2_plane[:].bitcast(I32), 0)
        nc.gpsimd.memset(xs_plane[:].bitcast(I32), 0)
        nc.vector.memset(warm[:], 0.0)
        nc.vector.memset(table_scales[:].bitcast(I32), 0)
        make_identity(nc, identity[:])
        nc.scalar.activation(warm_out[:], warm[:], ACT.Sin)

        raw = {}

        def load_table(a, half):
            cols = slice(half * T // 2, (half + 1) * T // 2)
            nc.sync.dma_start(table[a][:, cols], tab_words[a].rearrange("p n t -> p (n t)").bitcast(I32)[:, cols])

        def load_weight(name, w, b, a, pieces=1):
            width = HALF // pieces
            rows = w[a * K_PASS : (a + 1) * K_PASS, b * HALF : (b + 1) * HALF].rearrange("(p j) c -> p j c", j=PACK)
            for piece in range(pieces):
                tile = keep.tile([P, PACK, width], F32, name=f"{name}_raw{b}{a}{piece}")
                nc.sync.dma_start(tile[:], rows[:, :, piece * width : (piece + 1) * width])
                for half in range(piece, 2, pieces):
                    raw[name, b, a, half] = tile[:] if name == "w3" or pieces == 2 else tile[:, :, half * HALF // 2 : (half + 1) * HALF // 2]

        def load_stream_scales(q):
            nc.sync.dma_start(w2_plane[32 * q : 32 * q + 4, :].bitcast(I32), w2_scales[0, 4 * q : 4 * q + 4, :].bitcast(I32))
            nc.sync.dma_start(xs_plane[32 * q : 32 * q + 4, :].bitcast(I32), xs_scales[0, 4 * q : 4 * q + 4, :].bitcast(I32))

        nc.sync.dma_start(phase_dealt[:], phase.rearrange("(b p t) -> p b t", p=P, t=PACK))
        load_stream_scales(0)
        nc.sync.dma_start(w2_codes[:].bitcast(I32), w2_words[0].bitcast(I32))
        nc.sync.dma_start(xs_codes[:], xs_words[0].rearrange("p n t -> p (n t)").bitcast(I32))
        for q in range(1, 4):
            load_stream_scales(q)
        load_table(0, 0)
        nc.sync.dma_start(offsets[:], offs)
        load_table(0, 1)
        for q in range(4):
            nc.sync.dma_start(table_scales[32 * q : 32 * q + 8, :].bitcast(I32), tab_scales[:, 4 * q : 4 * q + 4, :].bitcast(I32))
        load_table(1, 0)
        load_table(1, 1)
        load_weight("w1", w1, 0, 0, pieces=2)
        nc.sync.dma_start(gain_sb[:], gain.rearrange("(b p t) -> p b t", p=P, t=PACK))
        load_weight("w1", w1, 0, 1, pieces=2)
        for a in range(2):
            load_weight("w1", w1, 1, a)
        for a in range(2):
            load_weight("w3", w3, 0, a)

        rounded, codes, planes = {}, {}, {}
        later = [(name, b, a, half) for name, b in (("w1", 1), ("w3", 0)) for a in range(2) for half in range(2)]
        joint = keep.tile([P, HALF * PACK], BF16, name="joint", align_bytes=64)
        for half in range(2):
            rounded[later[half]] = joint[:, half * 2 * HALF : (half + 1) * 2 * HALF].rearrange("p (c j) -> p c j", j=PACK)
        rounded["w1", 0, 0, 0] = rounded[later[0]]
        for name, b, a in sorted({key[:3] for key in raw}):
            codes[name, b, a] = keep.tile([P, HALF], U32, name=f"codes_{name}{b}{a}", align_bytes=64)
            planes[name, b, a] = keep.tile([P, HALF], U8, name=f"plane_{name}{b}{a}", align_bytes=64)

        def round_weight(key, tag, copy=nc.scalar.copy):
            if key not in rounded:
                rounded[key] = work.tile([P, HALF // 2, PACK], BF16, name="rounded", tag=tag, bufs=1, align_bytes=64)
            src = raw[key].rearrange("p j (m t) -> p m j t", t=PACK)
            if key[0] == "w3":
                src = src[:, :, :, 2 * key[3] : 2 * key[3] + 2]
                dst = rounded[key][:].rearrange("p (t m) j -> p m j t", t=2)
            else:
                dst = rounded[key][:].rearrange("p (m t) j -> p m j t", t=PACK)
            copy(dst, src)

        def quantize_weight(key):
            cols = slice(key[3] * HALF // 2, (key[3] + 1) * HALF // 2)
            if key == later[0]:
                return
            if key == later[1]:
                nc.vector.quantize_mx(
                    out=codes[key[:3]][:].bitcast(E4M3), scales=planes[key[:3]][:], in_=joint[:]
                )
                return
            nc.vector.quantize_mx(
                out=codes[key[:3]][:, cols].bitcast(E4M3),
                scales=planes[key[:3]][:, cols],
                in_=rounded[key][:].rearrange("p c j -> p (c j)"),
            )

        def bank(kind, index):
            return psum.tile([P, HALF], F32, name="bank", tag=f"{kind}{index}")

        chunks = S // CUES
        units = [(0, c) for c in range(LEAD)]
        behind = 0
        for c in range(LEAD, chunks + 1):
            catch_up = min(behind + 2, c)
            units.extend((1, k) for k in range(behind, catch_up))
            behind = catch_up
            if c < chunks:
                units.append((0, c))
        n = len(units)

        minus_phase = keep.tile([P, 2, HALF], F32, name="minus_phase")
        spread = [bank("y", b) for b in range(2)]
        for b in range(2):
            for t in range(PACK):
                nc.tensor.transpose(spread[b][:, t * P : (t + 1) * P], phase_dealt[:, b, t : t + 1].to_broadcast([P, P]), identity[:])
            nc.scalar.activation(minus_phase[:, b], spread[b][:], ACT.Copy, scale=-1.0)

        picked_plane = keep.tile([P, S], U8, name="picked_plane", align_bytes=64)
        picked = [keep.tile([P, S], I32, name=f"picked{a}", align_bytes=64) for a in range(2)]

        minus_b = {}
        for i in range(n):
            minus_b[units[i]] = keep.tile([P, PACK, P], F32, name=f"minus_b{i}")
        on_vector = [u for u in units if u[0] == 0 or u[1] < PACK]

        def subtract_b(i):
            b, c = on_vector[i]
            cols = slice(c * CUES, (c + 1) * CUES)
            b_bank = bank("a", i % 3)
            nc.tensor.matmul_mx(
                out=b_bank[:],
                lhsT=xs_codes[:, cols].bitcast(E4M3),
                lhsT_scale=xs_plane[:, cols],
                rhs=w2_codes[:, 2 * HALF * b : 2 * HALF * (b + 1)].bitcast(E2M1),
                rhs_scale=w2_plane[:, HALF * b : HALF * (b + 1)],
                start=True,
                stop=True,
            )
            nc.vector.tensor_tensor(
                minus_b[b, c][:],
                minus_phase[:, b].rearrange("p (t m) -> p t m", t=PACK),
                b_bank[:].rearrange("p (m t) -> p t m", t=PACK),
                ALU.subtract,
            )

        for i in range(FIRST_B):
            subtract_b(i)
        phase_row = work.tile([P, P, PACK], F32, name="phase_row", tag="staged3", bufs=1, align_bytes=64)
        nc.scalar.copy(phase_row[:], spread[1][:].rearrange("p (t m) -> p m t", t=PACK))
        turned = bank("h", 2)
        for g in range(PACK):
            nc.tensor.transpose(turned[:, g * P : (g + 1) * P], phase_row[:].rearrange("p m t -> p (m t)")[:, g * P : (g + 1) * P], identity[:])
        nc.scalar.copy(phase_rows[:], turned[:].rearrange("p (g m) -> p g m", g=PACK)[:, :, 0])

        nc.vector.tensor_copy(picked[0][:].bitcast(U32), table[0][:].bitcast(U32).indirect(offsets[:]))
        nc.vector.tensor_copy(picked_plane[:], table_scales[:].indirect(offsets[:]))
        nc.vector.tensor_copy(picked[1][:].bitcast(U32), table[1][:].bitcast(U32).indirect(offsets[:]))
        for half in range(1, 2):
            cols = slice(half * HALF, (half + 1) * HALF)
            by_channel = {}
            for g in range(PACK):
                first = HALF + g * P
                b_bank = bank("y", (g + 1) % 2)
                nc.tensor.matmul_mx(
                    out=b_bank[:],
                    lhsT=w2_codes[:, 2 * first : 2 * (first + P)].bitcast(E2M1),
                    lhsT_scale=w2_plane[:, first : first + P],
                    rhs=xs_codes[:, cols].bitcast(E4M3),
                    rhs_scale=xs_plane[:, cols],
                    start=True,
                    stop=True,
                )
                if g == 0:
                    by_channel[g] = joint[:, : 2 * HALF].bitcast(F32)
                else:
                    by_channel[g] = work.tile([P, HALF], F32, name="by_channel", tag=f"staged{g}", bufs=1, align_bytes=64)
                nc.scalar.activation(by_channel[g][:], b_bank[:], ACT.Identity, bias=phase_rows[:, g : g + 1])
            for k in range(PACK):
                turned = bank("h", (half * PACK + k) % 3)
                for g in range(PACK):
                    nc.tensor.transpose(turned[:, g * P : (g + 1) * P], by_channel[g][:, k * CUES : (k + 1) * CUES], identity[:])
                nc.scalar.activation(
                    minus_b[1, half * PACK + k][:], turned[:].rearrange("p (m t) -> p t m", t=PACK), ACT.Copy, scale=-1.0
                )

        rounded["w1", 0, 1, 1] = keep.tile([P, HALF // 2, PACK], BF16, name="rounded_last", tag="table1", align_bytes=64)
        for a in range(2):
            for half in range(2):
                round_weight(("w1", 0, a, half), f"staged{2 * a + half}", nc.vector.tensor_copy if (a, half) == (1, 1) else nc.scalar.copy)
                quantize_weight(("w1", 0, a, half))

        for i in range(FIRST_B, len(on_vector)):
            subtract_b(i)

        a_bank, z, whole, frac, sine, h_bank, h_bf = {}, {}, {}, {}, {}, {}, {}
        h_codes = [keep.tile([P, S], U32, name=f"h_codes{b}", align_bytes=64) for b in range(2)]
        h_plane = [keep.tile([P, S], U8, name=f"h_plane{b}", align_bytes=64) for b in range(2)]
        y_codes = keep.tile([P, S], I32, name="y_codes", align_bytes=64)
        y_plane = keep.tile([P, S], U8, name="y_plane", align_bytes=64)
        y_bf, y_sb, a_sb = {}, {}, {}
        out_rows = out_0.rearrange("(p t) j -> p t j", t=PACK)
        out_words = out_1[0].rearrange("p m t -> p (m t)").bitcast(I32)

        def product_a(i):
            b, c = units[i]
            cols = slice(c * CUES, (c + 1) * CUES)
            a_bank[i] = bank("a", i % 3)
            for a in range(2):
                nc.tensor.matmul_mx(
                    out=a_bank[i][:],
                    lhsT=picked[a][:, cols].bitcast(E4M3),
                    lhsT_scale=picked_plane[4 * a :, cols],
                    rhs=codes["w1", b, a][:].bitcast(E4M3),
                    rhs_scale=planes["w1", b, a][:],
                    start=(a == 0),
                    stop=(a == 1),
                )

        def angle(i):
            z[i] = work.tile([P, PACK, P], F32, name="z", tag="z", bufs=5)
            dealt = a_bank[i][:].rearrange("p (m t) -> p t m", t=PACK)
            nc.vector.tensor_tensor(z[i][:], dealt, minus_b[units[i]][:], ALU.subtract)
            if i >= COPY_A_FROM:
                a_sb[i] = work.tile([P, PACK, P], F32, name="a_sb", tag="a_sb", bufs=3)
                nc.scalar.copy(a_sb[i][:], dealt)

        def count_turns(i):
            if i == 0:
                whole[i] = joint[:, 2 * HALF :].bitcast(I32)
            elif i < len(later) - 1:
                whole[i] = work.tile([P, HALF], I32, name="whole", tag=f"early{i}", bufs=1, align_bytes=64)
            else:
                whole[i] = work.tile([P, HALF], I32, name="whole", tag="whole", bufs=2)
            nc.vector.tensor_scalar(whole[i][:], z[i][:].rearrange("p t m -> p (t m)"), 1.0 / TURN, None, ALU.mult)

        def reduce_angle(i):
            frac[i] = work.tile([P, HALF], F32, name="frac", tag="frac")
            sine[i] = work.tile([P, PACK, P], F32, name="sine", tag="sine")
            nc.vector.scalar_tensor_tensor(
                frac[i][:], z[i][:].rearrange("p t m -> p (t m)"), 1.0 / TURN, whole[i][:], ALU.mult, ALU.subtract
            )
            nc.scalar.activation(sine[i][:].rearrange("p t m -> p (t m)"), frac[i][:], ACT.Sin, scale=TURN)

        def turn_and_add(i):
            h_bank[i] = bank("h", i % 3)
            terms = (sine[i], a_sb[i]) if i >= COPY_A_FROM else (sine[i], z[i], minus_b[units[i]])
            for number, term in enumerate(terms):
                for t in range(PACK):
                    nc.tensor.matmul(
                        h_bank[i][:, t * P : (t + 1) * P],
                        term[:, t],
                        identity[:],
                        start=(number == 0 and t == 0),
                        stop=(number == len(terms) - 1 and t == PACK - 1),
                        is_transpose=True,
                    )

        def apply_gain(i):
            b, c = units[i]
            h_bf[i] = work.tile([P, CUES, PACK], BF16, name="h_bf", tag="h_bf", align_bytes=64)
            if i in GAIN_ON_SCALAR:
                by_slot = work.tile([P, PACK, CUES], BF16, name="by_slot", tag="by_slot", bufs=2)
                for t in range(PACK):
                    nc.scalar.activation(by_slot[:, t], h_bank[i][:, t * P : (t + 1) * P], ACT.Copy, scale=gain_sb[:, b, t : t + 1])
                nc.scalar.copy(
                    h_bf[i][:].rearrange("p (n i) t -> p n t i", i=PACK), by_slot[:].rearrange("p t (n i) -> p n t i", i=PACK)
                )
            else:
                gains = gain_sb[:, b].unsqueeze(1).to_broadcast([P, CUES, PACK])
                nc.vector.tensor_tensor(h_bf[i][:], h_bank[i][:].rearrange("p (t n) -> p n t", t=PACK), gains, ALU.mult)

        def quantize_h(i):
            b, c = units[i]
            cols = slice(c * CUES, (c + 1) * CUES)
            nc.vector.quantize_mx(
                out=h_codes[b][:, cols].bitcast(E4M3), scales=h_plane[b][:, cols], in_=h_bf[i][:].rearrange("p n t -> p (n t)")
            )

        def product_y(c):
            cols = slice(c * CUES, (c + 1) * CUES)
            y_bank = bank("y", c % 2)
            for a in range(2):
                for t in range(PACK):
                    w_cols = slice(t * P, (t + 1) * P)
                    nc.tensor.matmul_mx(
                        out=y_bank[:, w_cols],
                        lhsT=codes["w3", 0, a][:, w_cols].bitcast(E4M3),
                        lhsT_scale=planes["w3", 0, a][:, w_cols],
                        rhs=h_codes[a][:, cols].bitcast(E4M3),
                        rhs_scale=h_plane[a][:, cols],
                        start=(a == 0 and t == 0),
                        stop=(a == 1 and t == PACK - 1),
                    )
            y_bf[c] = work.tile([P, CUES, PACK], BF16, name="y_bf", tag="y_bf", align_bytes=64)
            if c < ROUND_ON_VECTOR_FROM:
                nc.scalar.copy(y_bf[c][:], y_bank[:].rearrange("p (t n) -> p n t", t=PACK))
            y_sb[c] = work.tile([P, PACK, CUES], F32, name="y_sb", tag="y_sb")
            nc.scalar.copy(y_sb[c][:].rearrange("p t n -> p (t n)"), y_bank[:])
            nc.sync.dma_start(out_rows[:, :, cols], y_sb[c][:])

        def round_y(c):
            nc.vector.tensor_copy(
                y_bf[c][:].rearrange("p (n i) t -> p n t i", i=PACK), y_sb[c][:].rearrange("p t (n i) -> p n t i", i=PACK)
            )

        def quantize_y(c):
            cols = slice(c * CUES, (c + 1) * CUES)
            nc.vector.quantize_mx(
                out=y_codes[:, cols].bitcast(E4M3), scales=y_plane[:, cols], in_=y_bf[c][:].rearrange("p n t -> p (n t)")
            )
            if c % 2 == 1:
                pair = slice((c - 1) * CUES, (c + 1) * CUES)
                nc.sync.dma_start(out_words[:, pair], y_codes[:, pair])

        product_a(0)
        for step in range(n + 8):
            if 2 <= step <= len(later):
                quantize_weight(later[step - 1])
            if step + 1 < n:
                product_a(step + 1)
            if step < n:
                angle(step)
            if 0 <= step - LAG - 1 < n:
                quantize_h(step - LAG - 1)
                if units[step - LAG - 1][0] == 1:
                    product_y(units[step - LAG - 1][1])
            if 0 <= step - LAG - 2 < n and units[step - LAG - 2][0] == 1 and units[step - LAG - 2][1] >= ROUND_ON_VECTOR_FROM:
                round_y(units[step - LAG - 2][1])
            if 0 <= step - LAG - 3 < n and units[step - LAG - 3][0] == 1:
                quantize_y(units[step - LAG - 3][1])
            if 0 <= step - 1 < n:
                reduce_angle(step - 1)
            if step == 1:
                round_weight(later[0], None)
            if 1 <= step < len(later):
                round_weight(later[step], f"early{step - 1}")
            if 0 <= step - 2 < n:
                turn_and_add(step - 2)
            if 0 <= step - LAG < n:
                apply_gain(step - LAG)
            if step < n:
                count_turns(step)
        for q in range(4):
            queue = nc.sync if q % 2 == 0 else nc.scalar
            queue.dma_start(out_2[0, 4 * q : 4 * q + 4, :].bitcast(I32), y_plane[32 * q : 32 * q + 4, :].bitcast(I32))
